import numpy as np
import ml_dtypes


def mxq(x, axis, fmt="e4m3"):
    dtype, down = {"e4m3": (ml_dtypes.float8_e4m3fn, 7), "e5m2": (ml_dtypes.float8_e5m2, 14)}[fmt]
    v = np.moveaxis(np.asarray(x, np.float32).astype(ml_dtypes.bfloat16).astype(np.float64), axis, -1)
    blocks = v.reshape(v.shape[:-1] + (-1, 32))
    amax = np.abs(blocks).max(-1, keepdims=True)
    byte = np.maximum(np.where(amax > 0, np.frexp(amax)[1] - 1 + 127, 0) - down, 1)
    scale = np.exp2(byte - 127.0)
    codes = (blocks / scale).astype(np.float32).astype(dtype).astype(np.float64)
    return np.moveaxis((codes * scale).reshape(v.shape), -1, axis)


WIDE = False


def mx_kscale(k):
    if not WIDE:
        return np.ones(k)
    levels = np.array([10, -10, 5, -5, 0])
    if k % 512:
        return np.exp2(np.random.permutation(np.resize(levels, k // 32))).repeat(32)
    a = np.empty((k // 512, 16))
    for p in range(k // 512):
        a[p, :8] = np.random.permutation(np.resize(levels, 8))
        for g in range(8):
            far = levels[np.abs(levels - a[p, g]) >= 10]
            a[p, g + 8] = far[np.random.randint(len(far))]
    return np.exp2(a.ravel()).repeat(32)


def f64(x):
    return np.asarray(x).astype(np.float64)


def striped(idx):
    return np.tile(idx.reshape(-1, 16).T, (8, 1)).astype(np.uint16)


def unstriped(offs):
    return offs[:16].T.reshape(-1).astype(np.int64)


E2M1 = np.array([0.0, 0.5, 1.0, 1.5, 2.0, 3.0, 4.0, 6.0, -0.0, -0.5, -1.0, -1.5, -2.0, -3.0, -4.0, -6.0])


def pack_weight(w, fmt):
    k, n = w.shape
    w = f64(np.asarray(w, np.float32).astype(ml_dtypes.bfloat16)).reshape(k // 32, 32, n)
    amax = np.abs(w).max(1)
    if fmt == "e4m3":
        byte = np.frexp(amax)[1] - 1 + 127 - 7
    else:
        mant, ex = np.frexp(amax / 6.0)
        byte = np.where(mant > 0.5, ex, ex - 1) + 127
    byte = np.clip(np.where(amax > 0, byte, 1), 1, 254)
    scaled = (w * np.exp2(127.0 - byte)[:, None, :]).reshape(k, n).astype(np.float32)
    by_word = np.ascontiguousarray(scaled.reshape(k // 512, 128, 4, n).transpose(0, 1, 3, 2))
    if fmt == "e4m3":
        words = by_word.astype(ml_dtypes.float8_e4m3fn).view(np.uint8)
    else:
        c = by_word.astype(ml_dtypes.float4_e2m1fn).view(np.uint8) & 0xF
        words = (c[..., 0::2] | (c[..., 1::2] << 4)).reshape(k // 512, 128, 2 * n)
    return np.ascontiguousarray(words), np.ascontiguousarray(byte.astype(np.uint8).reshape(k // 512, 16, n))


def unpack_weight(words, scales, fmt):
    g, _, n = scales.shape
    words = np.ascontiguousarray(words).reshape(g, 128, n, -1)
    if fmt == "e4m3":
        vals = words.view(ml_dtypes.float8_e4m3fn).astype(np.float64)
    else:
        nib = np.empty((g, 128, n, 4), np.uint8)
        nib[..., 0::2] = words & 0xF
        nib[..., 1::2] = words >> 4
        vals = E2M1[nib]
    vals = vals * np.repeat(np.exp2(scales.astype(np.float64) - 127.0), 8, axis=1)[..., None]
    return vals.transpose(0, 1, 3, 2).reshape(g * 512, n)


def gelu(v):
    return 0.5 * v * (1.0 + np.tanh(np.sqrt(2.0 / np.pi) * (v + 0.044715 * v**3)))


K, H, N, T, S, T2, P = 1024, 1024, 768, 2048, 512, 1024, 512

def setup_inputs():
    n = np.random.standard_normal
    s, u = mx_kscale(K)[:, None], mx_kscale(H)[:, None]
    tab_words, tab_scales = pack_weight(n((K, T)) * s, "e4m3")
    w4_words, w4_scales = pack_weight(1.1 * n((H, N)) / np.sqrt(H) / u, "e2m1")
    w5_words, w5_scales = pack_weight(n((K, N)) / np.sqrt(K) / s, "e4m3")
    return {
        "tab_words": tab_words, "tab_scales": tab_scales,
        "offs": striped(np.random.permutation(T)[:S]),
        "offs2": striped(np.random.permutation(T2)[:S]),
        "offs3": striped(np.random.permutation(T2)[:P]),
        "offs4": striped(np.random.permutation(T2)[:P]),
        "w1": (1.7 * n((K, H)) / np.sqrt(K) / s).astype(np.float32),
        "b1": (0.6 * n(H)).astype(np.float32),
        "gain": (np.random.uniform(0.8, 1.6, H) * u[:, 0]).astype(np.float32),
        "wgs": np.exp(0.3 * n((128, S))).astype(np.float32),
        "page0": (0.7 * n((H, T2)) * u).astype(np.float32),
        "w4_words": w4_words, "w4_scales": w4_scales,
        "w5_words": w5_words, "w5_scales": w5_scales,
    }

def reference(tab_words, tab_scales, offs, offs2, offs3, offs4, w1, b1, gain, wgs, page0,
              w4_words, w4_scales, w5_words, w5_scales):
    v = unpack_weight(tab_words, tab_scales, "e4m3")[:, unstriped(offs)]
    w4 = unpack_weight(w4_words, w4_scales, "e2m1")
    w5 = unpack_weight(w5_words, w5_scales, "e4m3")
    w1q = mxq(f64(w1), 0, "e4m3")
    h = f64(gain)[:, None] * np.tanh((w1q.T @ v) + f64(b1)[:, None])
    before = f64(page0)
    page = before.copy()
    page[:, unstriped(offs2)] = np.tile(f64(wgs), (H // 128, 1)) * h
    x = page[:, unstriped(offs3)] - before[:, unstriped(offs4)]
    xq = mxq(x, 0, "e4m3")
    return np.tanh(w4.T @ xq + w5.T @ v)

@@ -1,0 +1,235 @@
+from contextlib import ExitStack
+
+import concourse.mybir as mybir
+
+K, H, N, T, S, T2 = 1024, 1024, 768, 2048, 512, 1024
+FLOPS = 2 * K * H * S + 2 * H * N * S + 2 * K * N * S
+
+F32 = mybir.dt.float32
+BF16 = mybir.dt.bfloat16
+I32 = mybir.dt.int32
+U32 = mybir.dt.uint32
+U16 = mybir.dt.uint16
+U8 = mybir.dt.uint8
+FP8X4 = mybir.dt.float8_e4m3fn_x4
+FP4X4 = mybir.dt.float4_e2m1fn_x4
+ACT = mybir.ActivationFunctionType
+ALU = mybir.AluOpType
+
+P = 128
+PACK = 4
+PASS = P * PACK
+PASSES = 2
+SLICES = H // P
+QUADS = 4
+JQ = 128
+NQ = S // JQ
+TILES_A_BANK = 3
+HALVES = N // (P * TILES_A_BANK)
+
+
+def tile_list_fill_fouling_scores_kernel(
+    tc, tab_words, tab_scales, offs, offs2, offs3, offs4, w1, b1, gain, wgs, page0,
+    w4_words, w4_scales, w5_words, w5_scales, out,
+):
+    nc = tc.nc
+    with ExitStack() as ctx:
+        lists = ctx.enter_context(tc.tile_pool(name="lists", bufs=1))
+        keep = ctx.enter_context(tc.tile_pool(name="keep", bufs=1))
+        ring = ctx.enter_context(tc.tile_pool(name="ring", bufs=2))
+        psum = ctx.enter_context(tc.psum_pool(name="psum", bufs=1))
+
+        def held(shape, dtype, name):
+            return keep.tile(shape, dtype, name=name, align_bytes=64)
+
+        idx = lists.tile([P, S // 16], U16, name="idx")
+        idx2 = lists.tile([P, S // 16], U16, name="idx2")
+        idx3 = lists.tile([P, S // 16], U16, name="idx3")
+        idx4 = lists.tile([P, S // 16], U16, name="idx4")
+
+        tab_w = [held([P, T], I32, f"tab_w{a}") for a in range(PASSES)]
+        tab_s = held([P, T], U8, "tab_s")
+        v_w = [held([P, S], U32, f"v_w{a}") for a in range(PASSES)]
+        v_s = held([P, S], U8, "v_s")
+        w1_raw = [[held([P, PACK, PASS], F32, f"w1_raw{a}{b}") for b in range(PASSES)] for a in range(PASSES)]
+        w1_bf = [[held([P, PASS * PACK], BF16, f"w1_bf{a}{b}") for b in range(PASSES)] for a in range(PASSES)]
+        w1_w = [[held([P, PASS], U32, f"w1_w{a}{b}") for b in range(PASSES)] for a in range(PASSES)]
+        w1_s = [[held([P, PASS], U8, f"w1_s{a}{b}") for b in range(PASSES)] for a in range(PASSES)]
+        bias = held([P, PASSES, PACK], F32, "bias")
+        gains = held([P, PASSES, PACK], F32, "gains")
+        wgs_first = held([P, S], F32, "wgs_first")
+        wgs_rest = held([P, PACK - 1, S], F32, "wgs_rest")
+        page = [held([P, T2], F32, f"page{s}") for s in range(SLICES)]
+        before = [held([P, S], F32, f"before{s}") for s in range(SLICES)]
+        h = [held([P, S], F32, f"h{s}") for s in range(SLICES)]
+        x0 = held([P, PACK, S], F32, "x0")
+        x1_low = held([P, 2, S], F32, "x1_low")
+        x1_high = [held([P, 2, JQ], F32, f"x1_high{q}") for q in range(NQ)]
+        x0_w = held([P, S], U32, "x0_w")
+        x0_s = held([P, S], U8, "x0_s")
+        x1_bf = [held([P, JQ, PACK], BF16, f"x1_bf{q}") for q in range(NQ)]
+        x1_w = [held([P, JQ], U32, f"x1_w{q}") for q in range(NQ)]
+        x1_s = [held([P, JQ], U8, f"x1_s{q}") for q in range(NQ)]
+        w5_w = [held([P, N], I32, f"w5_w{a}") for a in range(PASSES)]
+        w4_w = [held([P, 2 * N], U8, f"w4_w{a}") for a in range(PASSES)]
+        w5_s = held([P, PASSES, N], U8, "w5_s")
+        w4_s = held([P, PASSES, N], U8, "w4_s")
+
+        nc.vector.memset(tab_s[:].bitcast(I32), 0)
+        nc.gpsimd.memset(w5_s[:].rearrange("p a n -> p (a n)").bitcast(I32), 0)
+        nc.gpsimd.memset(w4_s[:].rearrange("p a n -> p (a n)").bitcast(I32), 0)
+
+        def load_w1(a, b):
+            rows = w1[a * PASS:(a + 1) * PASS, b * PASS:(b + 1) * PASS]
+            nc.sync.dma_start(w1_raw[a][b][:], rows.rearrange("(p i) c -> p i c", i=PACK))
+
+        page_rows = page0.rearrange("(b p t) c -> b t p c", b=PASSES, t=PACK)
+
+        def load_page(s):
+            nc.sync.dma_start(page[s][:], page_rows[s // PACK, s % PACK])
+
+        def load_scale_rows(tile, scales):
+            for g in range(QUADS):
+                nc.sync.dma_start(
+                    tile[32 * g:32 * g + 4, :, :].bitcast(I32),
+                    scales[:, 4 * g:4 * g + 4, :].rearrange("a r n -> r a n").bitcast(I32),
+                )
+
+        wgs_rows = wgs.rearrange("(q t) j -> q t j", t=PACK)
+
+        load_w1(0, 0)
+        nc.sync.dma_start(idx[:], offs)
+        load_w1(1, 0)
+        for g in range(QUADS):
+            nc.sync.dma_start(
+                tab_s[32 * g:32 * g + 4 * PASSES, :].bitcast(I32),
+                tab_scales[:, 4 * g:4 * g + 4, :].bitcast(I32),
+            )
+        for a in range(PASSES):
+            nc.sync.dma_start(tab_w[a][:], tab_words[a].rearrange("p t i -> p (t i)").bitcast(I32))
+        nc.sync.dma_start(bias[:], b1.rearrange("(b p t) -> p b t", b=PASSES, t=PACK))
+        nc.sync.dma_start(gains[:], gain.rearrange("(b p t) -> p b t", b=PASSES, t=PACK))
+        nc.sync.dma_start(idx4[:], offs4)
+        nc.sync.dma_start(idx2[:], offs2)
+        load_page(0)
+        for g in range(QUADS):
+            nc.sync.dma_start(wgs_first[32 * g:32 * g + 32, :], wgs_rows[:, 0, :])
+        nc.sync.dma_start(idx3[:], offs3)
+        load_page(1)
+        for g in range(QUADS):
+            nc.sync.dma_start(wgs_rest[32 * g:32 * g + 32, :, :], wgs_rows[:, 1:PACK, :])
+        load_w1(0, 1)
+        load_w1(1, 1)
+        load_page(2)
+        for a in range(PASSES):
+            nc.sync.dma_start(w5_w[a][:], w5_words[a].rearrange("p n i -> p (n i)").bitcast(I32))
+        for a in range(PASSES):
+            nc.sync.dma_start(w4_w[a][:].bitcast(I32), w4_words[a].bitcast(I32))
+        for s in range(3, SLICES):
+            load_page(s)
+        load_scale_rows(w5_s, w5_scales)
+        load_scale_rows(w4_s, w4_scales)
+
+        def quantise_w1(a, b):
+            nc.scalar.copy(
+                w1_bf[a][b][:].rearrange("p (t m i) -> p m t i", t=PACK, i=PACK),
+                w1_raw[a][b][:].rearrange("p i (m t) -> p m t i", t=PACK),
+            )
+            nc.vector.quantize_mx(out=w1_w[a][b][:].bitcast(FP8X4), scales=w1_s[a][b][:], in_=w1_bf[a][b][:])
+
+        def make_h(s):
+            b, t = divmod(s, PACK)
+            acc = psum.tile([P, S], F32, name=f"bank{s}")
+            cols = slice(t * P, (t + 1) * P)
+            for a in range(PASSES):
+                nc.tensor.matmul_mx(
+                    out=acc[:], lhsT=w1_w[a][b][:, cols].bitcast(FP8X4), lhsT_scale=w1_s[a][b][:, cols],
+                    rhs=v_w[a][:].bitcast(FP8X4), rhs_scale=v_s[4 * a:P, :],
+                    start=(a == 0), stop=(a == PASSES - 1),
+                )
+            th = ring.tile([P, S], F32, name="scalar_ring", align_bytes=64)
+            nc.scalar.activation(th[:], acc[:], ACT.Tanh, bias=bias[:, b, t:t + 1])
+            nc.scalar.activation(h[s][:], th[:], ACT.Copy, scale=gains[:, b, t:t + 1])
+
+        def fetch_before(s):
+            nc.vector.tensor_copy(before[s][:], page[s][:].indirect(idx4[:]))
+
+        def put(s):
+            t = s % PACK
+            weight = wgs_first[:] if t == 0 else wgs_rest[:, t - 1, :]
+            nc.vector.tensor_tensor(page[s][:].indirect(idx2[:]), h[s][:], weight, ALU.mult)
+
+        def fetch_change(dst, s, j0, width):
+            nc.vector.tensor_tensor(
+                dst, page[s][:].indirect(idx3[:, j0 // 16:(j0 + width) // 16]), before[s][:, j0:j0 + width], ALU.subtract,
+            )
+
+        quantise_w1(0, 0)
+        nc.vector.tensor_copy(v_s[:], tab_s[:].indirect(idx[:]))
+        quantise_w1(1, 0)
+        for a in range(PASSES):
+            nc.vector.tensor_copy(v_w[a][:], tab_w[a][:].bitcast(U32).indirect(idx[:]))
+        for s in range(PACK):
+            make_h(s)
+        quantise_w1(0, 1)
+        quantise_w1(1, 1)
+        for s in range(PACK, SLICES):
+            make_h(s)
+
+        for s in range(SLICES):
+            fetch_before(s)
+            put(s)
+            if s < PACK:
+                fetch_change(x0[:, s, :], s, 0, S)
+            elif s < PACK + 2:
+                fetch_change(x1_low[:, s - PACK, :], s, 0, S)
+            if s == PACK - 1:
+                x0_bf = ring.tile([P, S, PACK], BF16, name="scalar_ring", align_bytes=64)
+                nc.scalar.copy(x0_bf[:], x0[:].rearrange("p t j -> p j t"))
+                nc.vector.quantize_mx(out=x0_w[:].bitcast(FP8X4), scales=x0_s[:], in_=x0_bf[:].rearrange("p j t -> p (j t)"))
+            if s == PACK + 1:
+                for q in range(NQ):
+                    nc.scalar.copy(x1_bf[q][:, :, 0:2], x1_low[:, :, q * JQ:(q + 1) * JQ].rearrange("p t j -> p j t"))
+
+        sums = {}
+        for q in range(NQ):
+            js = slice(q * JQ, (q + 1) * JQ)
+            for g in range(HALVES):
+                acc = psum.tile([P, TILES_A_BANK, JQ], F32, name=f"bank{HALVES * q + g}")
+                sums[q, g] = acc
+                for a in range(PASSES):
+                    for i in range(TILES_A_BANK):
+                        n0 = (g * TILES_A_BANK + i) * P
+                        nc.tensor.matmul_mx(
+                            out=acc[:, i, :], lhsT=w5_w[a][:, n0:n0 + P].bitcast(FP8X4), lhsT_scale=w5_s[:, a, n0:n0 + P],
+                            rhs=v_w[a][:, js].bitcast(FP8X4), rhs_scale=v_s[4 * a:P, js],
+                            start=(a == 0 and i == 0), stop=False,
+                        )
+        for q in range(NQ):
+            js = slice(q * JQ, (q + 1) * JQ)
+            for g in range(HALVES):
+                for i in range(TILES_A_BANK):
+                    n0 = (g * TILES_A_BANK + i) * P
+                    nc.tensor.matmul_mx(
+                        out=sums[q, g][:, i, :], lhsT=w4_w[0][:, 2 * n0:2 * (n0 + P)].bitcast(FP4X4), lhsT_scale=w4_s[:, 0, n0:n0 + P],
+                        rhs=x0_w[:, js].bitcast(FP8X4), rhs_scale=x0_s[:, js],
+                        start=False, stop=False,
+                    )
+
+        out_rows = out.rearrange("(g i p) j -> g p i j", g=HALVES, i=TILES_A_BANK)
+        for q in range(NQ):
+            for u in range(2):
+                fetch_change(x1_high[q][:, u, :], PACK + 2 + u, q * JQ, JQ)
+            nc.vector.tensor_copy(x1_bf[q][:, :, 2:4], x1_high[q][:].rearrange("p t j -> p j t"))
+            nc.vector.quantize_mx(out=x1_w[q][:].bitcast(FP8X4), scales=x1_s[q][:], in_=x1_bf[q][:].rearrange("p j t -> p (j t)"))
+            for g in range(HALVES):
+                for i in range(TILES_A_BANK):
+                    n0 = (g * TILES_A_BANK + i) * P
+                    nc.tensor.matmul_mx(
+                        out=sums[q, g][:, i, :], lhsT=w4_w[1][:, 2 * n0:2 * (n0 + P)].bitcast(FP4X4), lhsT_scale=w4_s[:, 1, n0:n0 + P],
+                        rhs=x1_w[q][:].bitcast(FP8X4), rhs_scale=x1_s[q][:],
+                        start=False, stop=(i == TILES_A_BANK - 1),
+                    )
+                scores = held([P, TILES_A_BANK, JQ], F32, f"scores{q}{g}")
+                nc.scalar.activation(scores[:], sums[q, g][:], ACT.Tanh)
+                nc.sync.dma_start(out_rows[g][:, :, q * JQ:(q + 1) * JQ], scores[:])

@@ -1,6 +1,7 @@
 from contextlib import ExitStack
 
 import concourse.mybir as mybir
+from concourse.masks import make_identity
 
 K, H, N, T, S, T2 = 1024, 1024, 768, 2048, 512, 1024
 FLOPS = 2 * K * H * S + 2 * H * N * S + 2 * K * N * S
@@ -26,6 +27,7 @@ JQ = 128
 NQ = S // JQ
 TILES_A_BANK = 3
 HALVES = N // (P * TILES_A_BANK)
+KIB = 1024
 
 
 def tile_list_fill_fouling_scores_kernel(
@@ -36,11 +38,14 @@ def tile_list_fill_fouling_scores_kernel(
     with ExitStack() as ctx:
         lists = ctx.enter_context(tc.tile_pool(name="lists", bufs=1))
         keep = ctx.enter_context(tc.tile_pool(name="keep", bufs=1))
-        ring = ctx.enter_context(tc.tile_pool(name="ring", bufs=2))
+        shared = ctx.enter_context(tc.tile_pool(name="shared", bufs=1))
         psum = ctx.enter_context(tc.psum_pool(name="psum", bufs=1))
 
         def held(shape, dtype, name):
             return keep.tile(shape, dtype, name=name, align_bytes=64)
+
+        def placed(kib, shape, dtype, name):
+            return shared.tile(shape, dtype, name=name, offset=int(kib * KIB), align_bytes=64)
 
         idx = lists.tile([P, S // 16], U16, name="idx")
         idx2 = lists.tile([P, S // 16], U16, name="idx2")
@@ -51,42 +56,50 @@ def tile_list_fill_fouling_scores_kernel(
         tab_s = held([P, T], U8, "tab_s")
         v_w = [held([P, S], U32, f"v_w{a}") for a in range(PASSES)]
         v_s = held([P, S], U8, "v_s")
-        w1_raw = [[held([P, PACK, PASS], F32, f"w1_raw{a}{b}") for b in range(PASSES)] for a in range(PASSES)]
-        w1_bf = [[held([P, PASS * PACK], BF16, f"w1_bf{a}{b}") for b in range(PASSES)] for a in range(PASSES)]
-        w1_w = [[held([P, PASS], U32, f"w1_w{a}{b}") for b in range(PASSES)] for a in range(PASSES)]
-        w1_s = [[held([P, PASS], U8, f"w1_s{a}{b}") for b in range(PASSES)] for a in range(PASSES)]
-        bias = held([P, PASSES, PACK], F32, "bias")
-        gains = held([P, PASSES, PACK], F32, "gains")
-        wgs_first = held([P, S], F32, "wgs_first")
-        wgs_rest = held([P, PACK - 1, S], F32, "wgs_rest")
+        identity = held([P, P], F32, "identity")
+        low_rows = held([P, P], F32, "low_rows")
+        low = held([P, 2 * PACK], F32, "low")
+        bias_high = held([P, PACK], F32, "bias_high")
+        gain_high = held([P, PACK], F32, "gain_high")
+        wgs_plain = held([P, S], F32, "wgs_plain")
+        wgs_dealt = held([P, PACK, S], F32, "wgs_dealt")
         page = [held([P, T2], F32, f"page{s}") for s in range(SLICES)]
-        before = [held([P, S], F32, f"before{s}") for s in range(SLICES)]
-        h = [held([P, S], F32, f"h{s}") for s in range(SLICES)]
-        x0 = held([P, PACK, S], F32, "x0")
-        x1_low = held([P, 2, S], F32, "x1_low")
-        x1_high = [held([P, 2, JQ], F32, f"x1_high{q}") for q in range(NQ)]
+        x0_bf = held([P, S, PACK], BF16, "x0_bf")
         x0_w = held([P, S], U32, "x0_w")
         x0_s = held([P, S], U8, "x0_s")
         x1_bf = [held([P, JQ, PACK], BF16, f"x1_bf{q}") for q in range(NQ)]
         x1_w = [held([P, JQ], U32, f"x1_w{q}") for q in range(NQ)]
         x1_s = [held([P, JQ], U8, f"x1_s{q}") for q in range(NQ)]
-        w5_w = [held([P, N], I32, f"w5_w{a}") for a in range(PASSES)]
         w4_w = [held([P, 2 * N], U8, f"w4_w{a}") for a in range(PASSES)]
         w5_s = held([P, PASSES, N], U8, "w5_s")
         w4_s = held([P, PASSES, N], U8, "w4_s")
+        w1_raw = [
+            held([P, PASSES, PACK, P], F32, "w1_raw0"),
+            placed(0, [P, PASSES, PACK, P], F32, "w1_raw1"),
+            placed(10, [P, PASSES, PACK, 2 * P], F32, "w1_raw2"),
+        ]
+        w1_raw_high = [held([P, PACK, PASS], F32, "w1_raw_high0"), placed(24, [P, PACK, PASS], F32, "w1_raw_high1")]
+        w5_w = [None, held([P, N], I32, "w5_w1")]
 
-        nc.vector.memset(tab_s[:].bitcast(I32), 0)
-        nc.gpsimd.memset(w5_s[:].rearrange("p a n -> p (a n)").bitcast(I32), 0)
-        nc.gpsimd.memset(w4_s[:].rearrange("p a n -> p (a n)").bitcast(I32), 0)
+        nc.gpsimd.memset(tab_s[:].bitcast(I32), 0)
+        nc.vector.memset(low_rows[:], 0.0)
+        make_identity(nc, identity[:])
+        nc.vector.memset(w5_s[:].rearrange("p a n -> p (a n)").bitcast(I32), 0)
+        nc.vector.memset(w4_s[:].rearrange("p a n -> p (a n)").bitcast(I32), 0)
 
-        def load_w1(a, b):
-            rows = w1[a * PASS:(a + 1) * PASS, b * PASS:(b + 1) * PASS]
-            nc.sync.dma_start(w1_raw[a][b][:], rows.rearrange("(p i) c -> p i c", i=PACK))
+        def load_w1(dst, a, c0, c1):
+            nc.sync.dma_start(dst, w1[a * PASS:(a + 1) * PASS, c0:c1].rearrange("(p i) c -> p i c", i=PACK))
 
-        page_rows = page0.rearrange("(b p t) c -> b t p c", b=PASSES, t=PACK)
+        def load_w1_low(piece, c0, c1):
+            for a in range(PASSES):
+                load_w1(w1_raw[piece][:, a], a, c0, c1)
 
         def load_page(s):
-            nc.sync.dma_start(page[s][:], page_rows[s // PACK, s % PACK])
+            if s < PACK:
+                rows = page0[s * P:(s + 1) * P, :]
+            else:
+                rows = page0[PASS:H, :].rearrange("(p t) c -> t p c", t=PACK)[s - PACK]
+            nc.sync.dma_start(page[s][:], rows)
 
         def load_scale_rows(tile, scales):
             for g in range(QUADS):
@@ -95,68 +108,107 @@ def tile_list_fill_fouling_scores_kernel(
                     scales[:, 4 * g:4 * g + 4, :].rearrange("a r n -> r a n").bitcast(I32),
                 )
 
-        wgs_rows = wgs.rearrange("(q t) j -> q t j", t=PACK)
+        def load_words(dst, words):
+            nc.sync.dma_start(dst[:], words.rearrange("p c i -> p (c i)").bitcast(I32))
 
-        load_w1(0, 0)
-        nc.sync.dma_start(idx[:], offs)
-        load_w1(1, 0)
+        for tile, source in ((idx, offs), (idx4, offs4), (idx2, offs2), (idx3, offs3)):
+            nc.sync.dma_start(tile[:], source)
+        nc.sync.dma_start(bias_high[:], b1[PASS:H].rearrange("(p t) -> p t", t=PACK))
+        nc.sync.dma_start(gain_high[:], gain[PASS:H].rearrange("(p t) -> p t", t=PACK))
+        load_w1_low(0, 0, P)
+        load_words(tab_w[0], tab_words[0])
         for g in range(QUADS):
             nc.sync.dma_start(
                 tab_s[32 * g:32 * g + 4 * PASSES, :].bitcast(I32),
                 tab_scales[:, 4 * g:4 * g + 4, :].bitcast(I32),
             )
-        for a in range(PASSES):
-            nc.sync.dma_start(tab_w[a][:], tab_words[a].rearrange("p t i -> p (t i)").bitcast(I32))
-        nc.sync.dma_start(bias[:], b1.rearrange("(b p t) -> p b t", b=PASSES, t=PACK))
-        nc.sync.dma_start(gains[:], gain.rearrange("(b p t) -> p b t", b=PASSES, t=PACK))
-        nc.sync.dma_start(idx4[:], offs4)
-        nc.sync.dma_start(idx2[:], offs2)
+        nc.sync.dma_start(low_rows[0:PACK, :], b1[0:PASS].rearrange("(s p) -> s p", p=P))
+        nc.sync.dma_start(low_rows[PACK:2 * PACK, :], gain[0:PASS].rearrange("(s p) -> s p", p=P))
+        load_words(tab_w[1], tab_words[1])
         load_page(0)
-        for g in range(QUADS):
-            nc.sync.dma_start(wgs_first[32 * g:32 * g + 32, :], wgs_rows[:, 0, :])
-        nc.sync.dma_start(idx3[:], offs3)
         load_page(1)
-        for g in range(QUADS):
-            nc.sync.dma_start(wgs_rest[32 * g:32 * g + 32, :, :], wgs_rows[:, 1:PACK, :])
-        load_w1(0, 1)
-        load_w1(1, 1)
+        nc.sync.dma_start(wgs_plain[:], wgs)
+        load_w1_low(1, P, 2 * P)
         load_page(2)
-        for a in range(PASSES):
-            nc.sync.dma_start(w5_w[a][:], w5_words[a].rearrange("p n i -> p (n i)").bitcast(I32))
+        load_page(3)
+        load_w1_low(2, 2 * P, PASS)
+        load_w1(w1_raw_high[0][:], 0, PASS, H)
+        load_page(4)
+        load_page(5)
+        load_w1(w1_raw_high[1][:], 1, PASS, H)
+        load_page(6)
+        load_page(7)
+        for g in range(QUADS):
+            nc.sync.dma_start(wgs_dealt[32 * g:32 * g + 32, :, :], wgs.rearrange("(q t) j -> q t j", t=PACK))
+        load_words(w5_w[1], w5_words[1])
         for a in range(PASSES):
             nc.sync.dma_start(w4_w[a][:].bitcast(I32), w4_words[a].bitcast(I32))
-        for s in range(3, SLICES):
-            load_page(s)
         load_scale_rows(w5_s, w5_scales)
         load_scale_rows(w4_s, w4_scales)
 
-        def quantise_w1(a, b):
-            nc.scalar.copy(
-                w1_bf[a][b][:].rearrange("p (t m i) -> p m t i", t=PACK, i=PACK),
-                w1_raw[a][b][:].rearrange("p i (m t) -> p m t i", t=PACK),
-            )
-            nc.vector.quantize_mx(out=w1_w[a][b][:].bitcast(FP8X4), scales=w1_s[a][b][:], in_=w1_bf[a][b][:])
+        turned = psum.tile([P, P], F32, name=f"bank{SLICES - 1}")
+        nc.tensor.transpose(turned[:], low_rows[:], identity[:])
+        nc.scalar.copy(low[:], turned[:, 0:2 * PACK])
 
-        def make_h(s):
-            b, t = divmod(s, PACK)
-            acc = psum.tile([P, S], F32, name=f"bank{s}")
-            cols = slice(t * P, (t + 1) * P)
+        stationary = {}
+
+        def quantise(rounded, name):
+            width = rounded.shape[1] // PACK
+            words = held([P, width], U32, f"{name}_w")
+            scales = held([P, width], U8, f"{name}_s")
+            nc.vector.quantize_mx(out=words[:].bitcast(FP8X4), scales=scales[:], in_=rounded[:])
+            return words, scales
+
+        def quantise_w1_low(piece, rounded, slices):
+            nc.scalar.copy(
+                rounded[:].rearrange("p (a c i) -> p a c i", a=PASSES, i=PACK),
+                w1_raw[piece][:].rearrange("p a i c -> p a c i"),
+            )
+            words, scales = quantise(rounded, f"w1_low{piece}")
             for a in range(PASSES):
+                for n, s in enumerate(slices):
+                    c0 = (a * len(slices) + n) * P
+                    stationary[s, a] = (words[:, c0:c0 + P], scales[:, c0:c0 + P])
+
+        def quantise_w1_high(a, rounded):
+            nc.scalar.copy(
+                rounded[:].rearrange("p (t m i) -> p m t i", t=PACK, i=PACK),
+                w1_raw_high[a][:].rearrange("p i (m t) -> p m t i", t=PACK),
+            )
+            words, scales = quantise(rounded, f"w1_high{a}")
+            for t in range(PACK):
+                stationary[PACK + t, a] = (words[:, t * P:(t + 1) * P], scales[:, t * P:(t + 1) * P])
+
+        tanh_of, h, before = {}, {}, {}
+
+        def first_product(s, th):
+            acc = psum.tile([P, S], F32, name=f"bank{s}")
+            for a in range(PASSES):
+                words, scales = stationary[s, a]
                 nc.tensor.matmul_mx(
-                    out=acc[:], lhsT=w1_w[a][b][:, cols].bitcast(FP8X4), lhsT_scale=w1_s[a][b][:, cols],
+                    out=acc[:], lhsT=words.bitcast(FP8X4), lhsT_scale=scales,
                     rhs=v_w[a][:].bitcast(FP8X4), rhs_scale=v_s[4 * a:P, :],
                     start=(a == 0), stop=(a == PASSES - 1),
                 )
-            th = ring.tile([P, S], F32, name="scalar_ring", align_bytes=64)
-            nc.scalar.activation(th[:], acc[:], ACT.Tanh, bias=bias[:, b, t:t + 1])
-            nc.scalar.activation(h[s][:], th[:], ACT.Copy, scale=gains[:, b, t:t + 1])
+            bias = low[:, s:s + 1] if s < PACK else bias_high[:, s - PACK:s - PACK + 1]
+            nc.scalar.activation(th[:], acc[:], ACT.Tanh, bias=bias)
+            tanh_of[s] = th
 
-        def fetch_before(s):
-            nc.vector.tensor_copy(before[s][:], page[s][:].indirect(idx4[:]))
+        def apply_gain(s, dst):
+            factor = low[:, PACK + s:PACK + s + 1] if s < PACK else gain_high[:, s - PACK:s - PACK + 1]
+            nc.scalar.activation(dst[:], tanh_of[s][:], ACT.Copy, scale=factor)
+            h[s] = dst
+
+        def make_h(s, th):
+            first_product(s, th)
+            apply_gain(s, held([P, S], F32, f"h{s}"))
+
+        def fetch_before(s, dst):
+            nc.vector.tensor_copy(dst[:], page[s][:].indirect(idx4[:]))
+            before[s] = dst
 
         def put(s):
-            t = s % PACK
-            weight = wgs_first[:] if t == 0 else wgs_rest[:, t - 1, :]
+            weight = wgs_plain[:] if s < PACK else wgs_dealt[:, s - PACK, :]
             nc.vector.tensor_tensor(page[s][:].indirect(idx2[:]), h[s][:], weight, ALU.mult)
 
         def fetch_change(dst, s, j0, width):
@@ -164,72 +216,96 @@ def tile_list_fill_fouling_scores_kernel(
                 dst, page[s][:].indirect(idx3[:, j0 // 16:(j0 + width) // 16]), before[s][:, j0:j0 + width], ALU.subtract,
             )
 
-        quantise_w1(0, 0)
+        x_rows = {}
+
+        def change_low(s, dst):
+            fetch_change(dst[:], s, 0, S)
+            x_rows[s] = dst
+
+        def row_tile(kib, name):
+            return placed(kib, [P, S], F32, name)
+
         nc.vector.tensor_copy(v_s[:], tab_s[:].indirect(idx[:]))
-        quantise_w1(1, 0)
+        quantise_w1_low(0, held([P, PASSES * P * PACK], BF16, "w1_bf0"), [0])
         for a in range(PASSES):
             nc.vector.tensor_copy(v_w[a][:], tab_w[a][:].bitcast(U32).indirect(idx[:]))
-        for s in range(PACK):
-            make_h(s)
-        quantise_w1(0, 1)
-        quantise_w1(1, 1)
+        make_h(0, held([P, S], F32, "turn0"))
+        fetch_before(0, held([P, S], F32, "before0"))
+        fetch_before(1, held([P, S], F32, "before1"))
+        put(0)
+        quantise_w1_low(1, held([P, PASSES * P * PACK], BF16, "turn0"), [1])
+        fetch_before(2, row_tile(0, "before2"))
+        fetch_before(3, row_tile(2, "before3"))
+        make_h(1, row_tile(5, "tanh1"))
+        put(1)
+        change_low(0, row_tile(4, "x_rows0"))
+        quantise_w1_low(2, placed(6, [P, PASSES * 2 * P * PACK], BF16, "w1_bf2"), [2, 3])
+        fetch_before(4, row_tile(10, "before4"))
+        fetch_before(5, row_tile(12, "before5"))
+        quantise_w1_high(0, placed(14, [P, PASS * PACK], BF16, "w1_bf_high0"))
+        make_h(2, row_tile(19, "tanh2"))
+        put(2)
+        change_low(1, row_tile(18, "x_rows1"))
+        quantise_w1_high(1, placed(20, [P, PASS * PACK], BF16, "w1_bf_high1"))
+        fetch_before(6, row_tile(24, "before6"))
+        fetch_before(7, row_tile(26, "before7"))
+        make_h(3, row_tile(28, "tanh3"))
         for s in range(PACK, SLICES):
-            make_h(s)
+            make_h(s, held([P, S], F32, f"turn{s}"))
+        put(3)
+        change_low(2, row_tile(28, "x_rows2"))
+        put(4)
+        change_low(3, held([P, S], F32, "turn4"))
 
-        for s in range(SLICES):
-            fetch_before(s)
+        x0 = placed(30, [P, PACK, S], F32, "x0")
+        w5_w[0] = placed(20, [P, N], I32, "w5_w0")
+        load_words(w5_w[0], w5_words[0])
+        for s in range(PACK):
+            for t in range(PACK):
+                nc.sync.dma_start(x0[32 * s:32 * s + 32, t, :], x_rows[s][t:P:PACK, :])
+        for s in range(PACK + 1, SLICES):
             put(s)
-            if s < PACK:
-                fetch_change(x0[:, s, :], s, 0, S)
-            elif s < PACK + 2:
-                fetch_change(x1_low[:, s - PACK, :], s, 0, S)
-            if s == PACK - 1:
-                x0_bf = ring.tile([P, S, PACK], BF16, name="scalar_ring", align_bytes=64)
-                nc.scalar.copy(x0_bf[:], x0[:].rearrange("p t j -> p j t"))
-                nc.vector.quantize_mx(out=x0_w[:].bitcast(FP8X4), scales=x0_s[:], in_=x0_bf[:].rearrange("p j t -> p (j t)"))
-            if s == PACK + 1:
-                for q in range(NQ):
-                    nc.scalar.copy(x1_bf[q][:, :, 0:2], x1_low[:, :, q * JQ:(q + 1) * JQ].rearrange("p t j -> p j t"))
+        nc.scalar.copy(x0_bf[:], x0[:].rearrange("p t j -> p j t"))
+        nc.vector.quantize_mx(out=x0_w[:].bitcast(FP8X4), scales=x0_s[:], in_=x0_bf[:].rearrange("p j t -> p (j t)"))
 
         sums = {}
         for q in range(NQ):
-            js = slice(q * JQ, (q + 1) * JQ)
             for g in range(HALVES):
-                acc = psum.tile([P, TILES_A_BANK, JQ], F32, name=f"bank{HALVES * q + g}")
-                sums[q, g] = acc
-                for a in range(PASSES):
-                    for i in range(TILES_A_BANK):
-                        n0 = (g * TILES_A_BANK + i) * P
-                        nc.tensor.matmul_mx(
-                            out=acc[:, i, :], lhsT=w5_w[a][:, n0:n0 + P].bitcast(FP8X4), lhsT_scale=w5_s[:, a, n0:n0 + P],
-                            rhs=v_w[a][:, js].bitcast(FP8X4), rhs_scale=v_s[4 * a:P, js],
-                            start=(a == 0 and i == 0), stop=False,
-                        )
+                sums[q, g] = psum.tile([P, TILES_A_BANK, JQ], F32, name=f"bank{HALVES * q + g}")
+
+        def add_pass(q, g, lhs_words, lhs_bytes, lhs_dtype, lhs_scales, rhs_words, rhs_scales, first=False, final=False):
+            for i in range(TILES_A_BANK):
+                n0 = (g * TILES_A_BANK + i) * P
+                nc.tensor.matmul_mx(
+                    out=sums[q, g][:, i, :],
+                    lhsT=lhs_words[:, lhs_bytes * n0:lhs_bytes * (n0 + P)].bitcast(lhs_dtype), lhsT_scale=lhs_scales[:, n0:n0 + P],
+                    rhs=rhs_words.bitcast(FP8X4), rhs_scale=rhs_scales,
+                    start=(first and i == 0), stop=(final and i == TILES_A_BANK - 1),
+                )
+
+        def add_direct(q, g, a):
+            js = slice(q * JQ, (q + 1) * JQ)
+            add_pass(q, g, w5_w[a], 1, FP8X4, w5_s[:, a, :], v_w[a][:, js], v_s[4 * a:P, js], first=(a == 0))
+
+        for q in range(NQ):
+            for g in range(HALVES):
+                add_direct(q, g, 0)
         for q in range(NQ):
             js = slice(q * JQ, (q + 1) * JQ)
             for g in range(HALVES):
-                for i in range(TILES_A_BANK):
-                    n0 = (g * TILES_A_BANK + i) * P
-                    nc.tensor.matmul_mx(
-                        out=sums[q, g][:, i, :], lhsT=w4_w[0][:, 2 * n0:2 * (n0 + P)].bitcast(FP4X4), lhsT_scale=w4_s[:, 0, n0:n0 + P],
-                        rhs=x0_w[:, js].bitcast(FP8X4), rhs_scale=x0_s[:, js],
-                        start=False, stop=False,
-                    )
+                add_pass(q, g, w4_w[0], 2, FP4X4, w4_s[:, 0, :], x0_w[:, js], x0_s[:, js])
+                add_direct(q, g, 1)
 
         out_rows = out.rearrange("(g i p) j -> g p i j", g=HALVES, i=TILES_A_BANK)
         for q in range(NQ):
-            for u in range(2):
-                fetch_change(x1_high[q][:, u, :], PACK + 2 + u, q * JQ, JQ)
-            nc.vector.tensor_copy(x1_bf[q][:, :, 2:4], x1_high[q][:].rearrange("p t j -> p j t"))
+            x1 = placed(32 + 2 * (q % 2), [P, PACK, JQ], F32, f"x1_{q}")
+            for t in range(PACK):
+                fetch_change(x1[:, t, :], PACK + t, q * JQ, JQ)
+            rounding_copy = nc.scalar.copy if q < NQ - 1 else nc.vector.tensor_copy
+            rounding_copy(x1_bf[q][:], x1[:].rearrange("p t j -> p j t"))
             nc.vector.quantize_mx(out=x1_w[q][:].bitcast(FP8X4), scales=x1_s[q][:], in_=x1_bf[q][:].rearrange("p j t -> p (j t)"))
             for g in range(HALVES):
-                for i in range(TILES_A_BANK):
-                    n0 = (g * TILES_A_BANK + i) * P
-                    nc.tensor.matmul_mx(
-                        out=sums[q, g][:, i, :], lhsT=w4_w[1][:, 2 * n0:2 * (n0 + P)].bitcast(FP4X4), lhsT_scale=w4_s[:, 1, n0:n0 + P],
-                        rhs=x1_w[q][:].bitcast(FP8X4), rhs_scale=x1_s[q][:],
-                        start=False, stop=(i == TILES_A_BANK - 1),
-                    )
+                add_pass(q, g, w4_w[1], 2, FP4X4, w4_s[:, 1, :], x1_w[q][:], x1_s[q][:], final=True)
                 scores = held([P, TILES_A_BANK, JQ], F32, f"scores{q}{g}")
                 nc.scalar.activation(scores[:], sums[q, g][:], ACT.Tanh)
                 nc.sync.dma_start(out_rows[g][:, :, q * JQ:(q + 1) * JQ], scores[:])

@@ -75,10 +75,10 @@ def tile_list_fill_fouling_scores_kernel(
         w4_s = held([P, PASSES, N], U8, "w4_s")
         w1_raw = [
             held([P, PASSES, PACK, P], F32, "w1_raw0"),
-            placed(0, [P, PASSES, PACK, P], F32, "w1_raw1"),
-            placed(10, [P, PASSES, PACK, 2 * P], F32, "w1_raw2"),
+            placed(1, [P, PASSES, PACK, P], F32, "w1_raw1"),
+            placed(13, [P, PASSES, PACK, 2 * P], F32, "w1_raw2"),
         ]
-        w1_raw_high = [held([P, PACK, PASS], F32, "w1_raw_high0"), placed(24, [P, PACK, PASS], F32, "w1_raw_high1")]
+        w1_raw_high = [held([P, PACK, PASS], F32, "w1_raw_high0"), placed(28, [P, PACK, PASS], F32, "w1_raw_high1")]
         w5_w = [None, held([P, N], I32, "w5_w1")]
 
         nc.gpsimd.memset(tab_s[:].bitcast(I32), 0)
@@ -129,15 +129,13 @@ def tile_list_fill_fouling_scores_kernel(
         load_page(1)
         nc.sync.dma_start(wgs_plain[:], wgs)
         load_w1_low(1, P, 2 * P)
-        load_page(2)
-        load_page(3)
+        for s in range(2, 5):
+            load_page(s)
         load_w1_low(2, 2 * P, PASS)
         load_w1(w1_raw_high[0][:], 0, PASS, H)
-        load_page(4)
-        load_page(5)
+        for s in range(5, SLICES):
+            load_page(s)
         load_w1(w1_raw_high[1][:], 1, PASS, H)
-        load_page(6)
-        load_page(7)
         for g in range(QUADS):
             nc.sync.dma_start(wgs_dealt[32 * g:32 * g + 32, :, :], wgs.rearrange("(q t) j -> q t j", t=PACK))
         load_words(w5_w[1], w5_words[1])
@@ -236,19 +234,19 @@ def tile_list_fill_fouling_scores_kernel(
         quantise_w1_low(1, held([P, PASSES * P * PACK], BF16, "turn0"), [1])
         fetch_before(2, row_tile(0, "before2"))
         fetch_before(3, row_tile(2, "before3"))
-        make_h(1, row_tile(5, "tanh1"))
+        fetch_before(4, row_tile(4, "before4"))
+        make_h(1, row_tile(7, "tanh1"))
         put(1)
-        change_low(0, row_tile(4, "x_rows0"))
-        quantise_w1_low(2, placed(6, [P, PASSES * 2 * P * PACK], BF16, "w1_bf2"), [2, 3])
-        fetch_before(4, row_tile(10, "before4"))
+        change_low(0, row_tile(6, "x_rows0"))
+        quantise_w1_low(2, placed(8, [P, PASSES * 2 * P * PACK], BF16, "w1_bf2"), [2, 3])
         fetch_before(5, row_tile(12, "before5"))
-        quantise_w1_high(0, placed(14, [P, PASS * PACK], BF16, "w1_bf_high0"))
-        make_h(2, row_tile(19, "tanh2"))
+        fetch_before(6, row_tile(14, "before6"))
+        fetch_before(7, row_tile(16, "before7"))
+        quantise_w1_high(0, placed(18, [P, PASS * PACK], BF16, "w1_bf_high0"))
+        make_h(2, row_tile(23, "tanh2"))
         put(2)
-        change_low(1, row_tile(18, "x_rows1"))
-        quantise_w1_high(1, placed(20, [P, PASS * PACK], BF16, "w1_bf_high1"))
-        fetch_before(6, row_tile(24, "before6"))
-        fetch_before(7, row_tile(26, "before7"))
+        change_low(1, row_tile(22, "x_rows1"))
+        quantise_w1_high(1, placed(24, [P, PASS * PACK], BF16, "w1_bf_high1"))
         make_h(3, row_tile(28, "tanh3"))
         for s in range(PACK, SLICES):
             make_h(s, held([P, S], F32, f"turn{s}"))
@@ -258,7 +256,7 @@ def tile_list_fill_fouling_scores_kernel(
         change_low(3, held([P, S], F32, "turn4"))
 
         x0 = placed(30, [P, PACK, S], F32, "x0")
-        w5_w[0] = placed(20, [P, N], I32, "w5_w0")
+        w5_w[0] = placed(24, [P, N], I32, "w5_w0")
         load_words(w5_w[0], w5_words[0])
         for s in range(PACK):
             for t in range(PACK):
@@ -283,9 +281,9 @@ def tile_list_fill_fouling_scores_kernel(
                     start=(first and i == 0), stop=(final and i == TILES_A_BANK - 1),
                 )
 
-        def add_direct(q, g, a):
+        def add_direct(q, g, a, final=False):
             js = slice(q * JQ, (q + 1) * JQ)
-            add_pass(q, g, w5_w[a], 1, FP8X4, w5_s[:, a, :], v_w[a][:, js], v_s[4 * a:P, js], first=(a == 0))
+            add_pass(q, g, w5_w[a], 1, FP8X4, w5_s[:, a, :], v_w[a][:, js], v_s[4 * a:P, js], first=(a == 0), final=final)
 
         for q in range(NQ):
             for g in range(HALVES):
@@ -294,7 +292,8 @@ def tile_list_fill_fouling_scores_kernel(
             js = slice(q * JQ, (q + 1) * JQ)
             for g in range(HALVES):
                 add_pass(q, g, w4_w[0], 2, FP4X4, w4_s[:, 0, :], x0_w[:, js], x0_s[:, js])
-                add_direct(q, g, 1)
+                if q >= NQ // 2:
+                    add_direct(q, g, 1)
 
         out_rows = out.rearrange("(g i p) j -> g p i j", g=HALVES, i=TILES_A_BANK)
         for q in range(NQ):
@@ -305,7 +304,9 @@ def tile_list_fill_fouling_scores_kernel(
             rounding_copy(x1_bf[q][:], x1[:].rearrange("p t j -> p j t"))
             nc.vector.quantize_mx(out=x1_w[q][:].bitcast(FP8X4), scales=x1_s[q][:], in_=x1_bf[q][:].rearrange("p j t -> p (j t)"))
             for g in range(HALVES):
-                add_pass(q, g, w4_w[1], 2, FP4X4, w4_s[:, 1, :], x1_w[q][:], x1_s[q][:], final=True)
+                add_pass(q, g, w4_w[1], 2, FP4X4, w4_s[:, 1, :], x1_w[q][:], x1_s[q][:], final=(q >= NQ // 2))
+                if q < NQ // 2:
+                    add_direct(q, g, 1, final=True)
                 scores = held([P, TILES_A_BANK, JQ], F32, f"scores{q}{g}")
                 nc.scalar.activation(scores[:], sums[q, g][:], ACT.Tanh)
                 nc.sync.dma_start(out_rows[g][:, :, q * JQ:(q + 1) * JQ], scores[:])

from contextlib import ExitStack

import concourse.mybir as mybir
from concourse.masks import make_identity

K, H, N, T, S, T2 = 1024, 1024, 768, 2048, 512, 1024
FLOPS = 2 * K * H * S + 2 * H * N * S + 2 * K * N * S

F32 = mybir.dt.float32
BF16 = mybir.dt.bfloat16
I32 = mybir.dt.int32
U32 = mybir.dt.uint32
U16 = mybir.dt.uint16
U8 = mybir.dt.uint8
FP8X4 = mybir.dt.float8_e4m3fn_x4
FP4X4 = mybir.dt.float4_e2m1fn_x4
ACT = mybir.ActivationFunctionType
ALU = mybir.AluOpType

P = 128
PACK = 4
PASS = P * PACK
PASSES = 2
SLICES = H // P
QUADS = 4
JQ = 128
NQ = S // JQ
TILES_A_BANK = 3
HALVES = N // (P * TILES_A_BANK)
KIB = 1024


def tile_list_fill_fouling_scores_kernel(
    tc, tab_words, tab_scales, offs, offs2, offs3, offs4, w1, b1, gain, wgs, page0,
    w4_words, w4_scales, w5_words, w5_scales, out,
):
    nc = tc.nc
    with ExitStack() as ctx:
        lists = ctx.enter_context(tc.tile_pool(name="lists", bufs=1))
        keep = ctx.enter_context(tc.tile_pool(name="keep", bufs=1))
        shared = ctx.enter_context(tc.tile_pool(name="shared", bufs=1))
        psum = ctx.enter_context(tc.psum_pool(name="psum", bufs=1))

        def held(shape, dtype, name):
            return keep.tile(shape, dtype, name=name, align_bytes=64)

        def placed(kib, shape, dtype, name):
            return shared.tile(shape, dtype, name=name, offset=int(kib * KIB), align_bytes=64)

        idx = lists.tile([P, S // 16], U16, name="idx")
        idx2 = lists.tile([P, S // 16], U16, name="idx2")
        idx3 = lists.tile([P, S // 16], U16, name="idx3")
        idx4 = lists.tile([P, S // 16], U16, name="idx4")

        tab_w = [held([P, T], I32, f"tab_w{a}") for a in range(PASSES)]
        tab_s = held([P, T], U8, "tab_s")
        v_w = [held([P, S], U32, f"v_w{a}") for a in range(PASSES)]
        v_s = held([P, S], U8, "v_s")
        identity = held([P, P], F32, "identity")
        low_rows = held([P, P], F32, "low_rows")
        low = held([P, 2 * PACK], F32, "low")
        bias_high = held([P, PACK], F32, "bias_high")
        gain_high = held([P, PACK], F32, "gain_high")
        wgs_plain = held([P, S], F32, "wgs_plain")
        wgs_dealt = held([P, PACK, S], F32, "wgs_dealt")
        page = [held([P, T2], F32, f"page{s}") for s in range(SLICES)]
        x0_bf = held([P, S, PACK], BF16, "x0_bf")
        x0_w = held([P, S], U32, "x0_w")
        x0_s = held([P, S], U8, "x0_s")
        x1_bf = [held([P, JQ, PACK], BF16, f"x1_bf{q}") for q in range(NQ)]
        x1_w = [held([P, JQ], U32, f"x1_w{q}") for q in range(NQ)]
        x1_s = [held([P, JQ], U8, f"x1_s{q}") for q in range(NQ)]
        w4_w = [held([P, 2 * N], U8, f"w4_w{a}") for a in range(PASSES)]
        w5_s = held([P, PASSES, N], U8, "w5_s")
        w4_s = held([P, PASSES, N], U8, "w4_s")
        w1_raw = [
            held([P, PASSES, PACK, P], F32, "w1_raw0"),
            placed(1, [P, PASSES, PACK, P], F32, "w1_raw1"),
            placed(13, [P, PASSES, PACK, 2 * P], F32, "w1_raw2"),
        ]
        w1_raw_high = [held([P, PACK, PASS], F32, "w1_raw_high0"), placed(28, [P, PACK, PASS], F32, "w1_raw_high1")]
        w5_w = [None, held([P, N], I32, "w5_w1")]

        nc.gpsimd.memset(tab_s[:].bitcast(I32), 0)
        nc.vector.memset(low_rows[:], 0.0)
        make_identity(nc, identity[:])
        nc.vector.memset(w5_s[:].rearrange("p a n -> p (a n)").bitcast(I32), 0)
        nc.vector.memset(w4_s[:].rearrange("p a n -> p (a n)").bitcast(I32), 0)

        def load_w1(dst, a, c0, c1):
            nc.sync.dma_start(dst, w1[a * PASS:(a + 1) * PASS, c0:c1].rearrange("(p i) c -> p i c", i=PACK))

        def load_w1_low(piece, c0, c1):
            for a in range(PASSES):
                load_w1(w1_raw[piece][:, a], a, c0, c1)

        def load_page(s):
            if s < PACK:
                rows = page0[s * P:(s + 1) * P, :]
            else:
                rows = page0[PASS:H, :].rearrange("(p t) c -> t p c", t=PACK)[s - PACK]
            nc.sync.dma_start(page[s][:], rows)

        def load_scale_rows(tile, scales):
            for g in range(QUADS):
                nc.sync.dma_start(
                    tile[32 * g:32 * g + 4, :, :].bitcast(I32),
                    scales[:, 4 * g:4 * g + 4, :].rearrange("a r n -> r a n").bitcast(I32),
                )

        def load_words(dst, words):
            nc.sync.dma_start(dst[:], words.rearrange("p c i -> p (c i)").bitcast(I32))

        for tile, source in ((idx, offs), (idx4, offs4), (idx2, offs2), (idx3, offs3)):
            nc.sync.dma_start(tile[:], source)
        nc.sync.dma_start(bias_high[:], b1[PASS:H].rearrange("(p t) -> p t", t=PACK))
        nc.sync.dma_start(gain_high[:], gain[PASS:H].rearrange("(p t) -> p t", t=PACK))
        load_w1_low(0, 0, P)
        load_words(tab_w[0], tab_words[0])
        for g in range(QUADS):
            nc.sync.dma_start(
                tab_s[32 * g:32 * g + 4 * PASSES, :].bitcast(I32),
                tab_scales[:, 4 * g:4 * g + 4, :].bitcast(I32),
            )
        nc.sync.dma_start(low_rows[0:PACK, :], b1[0:PASS].rearrange("(s p) -> s p", p=P))
        nc.sync.dma_start(low_rows[PACK:2 * PACK, :], gain[0:PASS].rearrange("(s p) -> s p", p=P))
        load_words(tab_w[1], tab_words[1])
        load_page(0)
        load_page(1)
        nc.sync.dma_start(wgs_plain[:], wgs)
        load_w1_low(1, P, 2 * P)
        for s in range(2, 5):
            load_page(s)
        load_w1_low(2, 2 * P, PASS)
        load_w1(w1_raw_high[0][:], 0, PASS, H)
        for s in range(5, SLICES):
            load_page(s)
        load_w1(w1_raw_high[1][:], 1, PASS, H)
        for g in range(QUADS):
            nc.sync.dma_start(wgs_dealt[32 * g:32 * g + 32, :, :], wgs.rearrange("(q t) j -> q t j", t=PACK))
        load_words(w5_w[1], w5_words[1])
        for a in range(PASSES):
            nc.sync.dma_start(w4_w[a][:].bitcast(I32), w4_words[a].bitcast(I32))
        load_scale_rows(w5_s, w5_scales)
        load_scale_rows(w4_s, w4_scales)

        turned = psum.tile([P, P], F32, name=f"bank{SLICES - 1}")
        nc.tensor.transpose(turned[:], low_rows[:], identity[:])
        nc.scalar.copy(low[:], turned[:, 0:2 * PACK])

        stationary = {}

        def quantise(rounded, name):
            width = rounded.shape[1] // PACK
            words = held([P, width], U32, f"{name}_w")
            scales = held([P, width], U8, f"{name}_s")
            nc.vector.quantize_mx(out=words[:].bitcast(FP8X4), scales=scales[:], in_=rounded[:])
            return words, scales

        def quantise_w1_low(piece, rounded, slices):
            nc.scalar.copy(
                rounded[:].rearrange("p (a c i) -> p a c i", a=PASSES, i=PACK),
                w1_raw[piece][:].rearrange("p a i c -> p a c i"),
            )
            words, scales = quantise(rounded, f"w1_low{piece}")
            for a in range(PASSES):
                for n, s in enumerate(slices):
                    c0 = (a * len(slices) + n) * P
                    stationary[s, a] = (words[:, c0:c0 + P], scales[:, c0:c0 + P])

        def quantise_w1_high(a, rounded):
            nc.scalar.copy(
                rounded[:].rearrange("p (t m i) -> p m t i", t=PACK, i=PACK),
                w1_raw_high[a][:].rearrange("p i (m t) -> p m t i", t=PACK),
            )
            words, scales = quantise(rounded, f"w1_high{a}")
            for t in range(PACK):
                stationary[PACK + t, a] = (words[:, t * P:(t + 1) * P], scales[:, t * P:(t + 1) * P])

        tanh_of, h, before = {}, {}, {}

        def first_product(s, th):
            acc = psum.tile([P, S], F32, name=f"bank{s}")
            for a in range(PASSES):
                words, scales = stationary[s, a]
                nc.tensor.matmul_mx(
                    out=acc[:], lhsT=words.bitcast(FP8X4), lhsT_scale=scales,
                    rhs=v_w[a][:].bitcast(FP8X4), rhs_scale=v_s[4 * a:P, :],
                    start=(a == 0), stop=(a == PASSES - 1),
                )
            bias = low[:, s:s + 1] if s < PACK else bias_high[:, s - PACK:s - PACK + 1]
            nc.scalar.activation(th[:], acc[:], ACT.Tanh, bias=bias)
            tanh_of[s] = th

        def apply_gain(s, dst):
            factor = low[:, PACK + s:PACK + s + 1] if s < PACK else gain_high[:, s - PACK:s - PACK + 1]
            nc.scalar.activation(dst[:], tanh_of[s][:], ACT.Copy, scale=factor)
            h[s] = dst

        def make_h(s, th):
            first_product(s, th)
            apply_gain(s, held([P, S], F32, f"h{s}"))

        def fetch_before(s, dst):
            nc.vector.tensor_copy(dst[:], page[s][:].indirect(idx4[:]))
            before[s] = dst

        def put(s):
            weight = wgs_plain[:] if s < PACK else wgs_dealt[:, s - PACK, :]
            nc.vector.tensor_tensor(page[s][:].indirect(idx2[:]), h[s][:], weight, ALU.mult)

        def fetch_change(dst, s, j0, width):
            nc.vector.tensor_tensor(
                dst, page[s][:].indirect(idx3[:, j0 // 16:(j0 + width) // 16]), before[s][:, j0:j0 + width], ALU.subtract,
            )

        x_rows = {}

        def change_low(s, dst):
            fetch_change(dst[:], s, 0, S)
            x_rows[s] = dst

        def row_tile(kib, name):
            return placed(kib, [P, S], F32, name)

        nc.vector.tensor_copy(v_s[:], tab_s[:].indirect(idx[:]))
        quantise_w1_low(0, held([P, PASSES * P * PACK], BF16, "w1_bf0"), [0])
        for a in range(PASSES):
            nc.vector.tensor_copy(v_w[a][:], tab_w[a][:].bitcast(U32).indirect(idx[:]))
        make_h(0, held([P, S], F32, "turn0"))
        fetch_before(0, held([P, S], F32, "before0"))
        fetch_before(1, held([P, S], F32, "before1"))
        put(0)
        quantise_w1_low(1, held([P, PASSES * P * PACK], BF16, "turn0"), [1])
        fetch_before(2, row_tile(0, "before2"))
        fetch_before(3, row_tile(2, "before3"))
        fetch_before(4, row_tile(4, "before4"))
        make_h(1, row_tile(7, "tanh1"))
        put(1)
        change_low(0, row_tile(6, "x_rows0"))
        quantise_w1_low(2, placed(8, [P, PASSES * 2 * P * PACK], BF16, "w1_bf2"), [2, 3])
        fetch_before(5, row_tile(12, "before5"))
        fetch_before(6, row_tile(14, "before6"))
        fetch_before(7, row_tile(16, "before7"))
        quantise_w1_high(0, placed(18, [P, PASS * PACK], BF16, "w1_bf_high0"))
        make_h(2, row_tile(23, "tanh2"))
        put(2)
        change_low(1, row_tile(22, "x_rows1"))
        quantise_w1_high(1, placed(24, [P, PASS * PACK], BF16, "w1_bf_high1"))
        make_h(3, row_tile(28, "tanh3"))
        for s in range(PACK, SLICES):
            make_h(s, held([P, S], F32, f"turn{s}"))
        put(3)
        change_low(2, row_tile(28, "x_rows2"))
        put(4)
        change_low(3, held([P, S], F32, "turn4"))

        x0 = placed(30, [P, PACK, S], F32, "x0")
        w5_w[0] = placed(24, [P, N], I32, "w5_w0")
        load_words(w5_w[0], w5_words[0])
        for s in range(PACK):
            for t in range(PACK):
                nc.sync.dma_start(x0[32 * s:32 * s + 32, t, :], x_rows[s][t:P:PACK, :])
        for s in range(PACK + 1, SLICES):
            put(s)
        nc.scalar.copy(x0_bf[:], x0[:].rearrange("p t j -> p j t"))
        nc.vector.quantize_mx(out=x0_w[:].bitcast(FP8X4), scales=x0_s[:], in_=x0_bf[:].rearrange("p j t -> p (j t)"))

        sums = {}
        for q in range(NQ):
            for g in range(HALVES):
                sums[q, g] = psum.tile([P, TILES_A_BANK, JQ], F32, name=f"bank{HALVES * q + g}")

        def add_pass(q, g, lhs_words, lhs_bytes, lhs_dtype, lhs_scales, rhs_words, rhs_scales, first=False, final=False):
            for i in range(TILES_A_BANK):
                n0 = (g * TILES_A_BANK + i) * P
                nc.tensor.matmul_mx(
                    out=sums[q, g][:, i, :],
                    lhsT=lhs_words[:, lhs_bytes * n0:lhs_bytes * (n0 + P)].bitcast(lhs_dtype), lhsT_scale=lhs_scales[:, n0:n0 + P],
                    rhs=rhs_words.bitcast(FP8X4), rhs_scale=rhs_scales,
                    start=(first and i == 0), stop=(final and i == TILES_A_BANK - 1),
                )

        def add_direct(q, g, a, final=False):
            js = slice(q * JQ, (q + 1) * JQ)
            add_pass(q, g, w5_w[a], 1, FP8X4, w5_s[:, a, :], v_w[a][:, js], v_s[4 * a:P, js], first=(a == 0), final=final)

        for q in range(NQ):
            for g in range(HALVES):
                add_direct(q, g, 0)
        for q in range(NQ):
            js = slice(q * JQ, (q + 1) * JQ)
            for g in range(HALVES):
                add_pass(q, g, w4_w[0], 2, FP4X4, w4_s[:, 0, :], x0_w[:, js], x0_s[:, js])
                if q >= NQ // 2:
                    add_direct(q, g, 1)

        out_rows = out.rearrange("(g i p) j -> g p i j", g=HALVES, i=TILES_A_BANK)
        for q in range(NQ):
            x1 = placed(32 + 2 * (q % 2), [P, PACK, JQ], F32, f"x1_{q}")
            for t in range(PACK):
                fetch_change(x1[:, t, :], PACK + t, q * JQ, JQ)
            rounding_copy = nc.scalar.copy if q < NQ - 1 else nc.vector.tensor_copy
            rounding_copy(x1_bf[q][:], x1[:].rearrange("p t j -> p j t"))
            nc.vector.quantize_mx(out=x1_w[q][:].bitcast(FP8X4), scales=x1_s[q][:], in_=x1_bf[q][:].rearrange("p j t -> p (j t)"))
            for g in range(HALVES):
                add_pass(q, g, w4_w[1], 2, FP4X4, w4_s[:, 1, :], x1_w[q][:], x1_s[q][:], final=(q >= NQ // 2))
                if q < NQ // 2:
                    add_direct(q, g, 1, final=True)
                scores = held([P, TILES_A_BANK, JQ], F32, f"scores{q}{g}")
                nc.scalar.activation(scores[:], sums[q, g][:], ACT.Tanh)
                nc.sync.dma_start(out_rows[g][:, :, q * JQ:(q + 1) * JQ], scores[:])
